import numpy as np
import ml_dtypes


def mxq(x, axis, fmt="e4m3"):
    dtype, down = {"e4m3": (ml_dtypes.float8_e4m3fn, 7), "e5m2": (ml_dtypes.float8_e5m2, 14)}[fmt]
    v = np.moveaxis(np.asarray(x, np.float32).astype(ml_dtypes.bfloat16).astype(np.float64), axis, -1)
    blocks = v.reshape(v.shape[:-1] + (-1, 32))
    amax = np.abs(blocks).max(-1, keepdims=True)
    byte = np.maximum(np.where(amax > 0, np.frexp(amax)[1] - 1 + 127, 0) - down, 1)
    scale = np.exp2(byte - 127.0)
    codes = (blocks / scale).astype(np.float32).astype(dtype).astype(np.float64)
    return np.moveaxis((codes * scale).reshape(v.shape), -1, axis)


WIDE = False


def mx_kscale(k):
    if not WIDE:
        return np.ones(k)
    levels = np.array([10, -10, 5, -5, 0])
    if k % 512:
        return np.exp2(np.random.permutation(np.resize(levels, k // 32))).repeat(32)
    a = np.empty((k // 512, 16))
    for p in range(k // 512):
        a[p, :8] = np.random.permutation(np.resize(levels, 8))
        for g in range(8):
            far = levels[np.abs(levels - a[p, g]) >= 10]
            a[p, g + 8] = far[np.random.randint(len(far))]
    return np.exp2(a.ravel()).repeat(32)


def f64(x):
    return np.asarray(x).astype(np.float64)


def striped(idx):
    return np.tile(idx.reshape(-1, 16).T, (8, 1)).astype(np.uint16)


def unstriped(offs):
    return offs[:16].T.reshape(-1).astype(np.int64)


def striped8(idx):
    return np.concatenate([x.reshape(-1, 16).T for x in idx]).astype(np.uint16)


def runs(offs, k):
    lists = np.stack([offs[16 * r : 16 * r + 16].T.reshape(-1) for r in range(8)]).astype(np.int64)
    return lists[np.arange(k) % 512 // 64]


def pack_weight(w):
    k, n = w.shape
    w = f64(np.asarray(w, np.float32).astype(ml_dtypes.bfloat16)).reshape(k // 32, 32, n)
    amax = np.abs(w).max(1)
    byte = np.clip(np.where(amax > 0, np.frexp(amax)[1] - 1 + 127 - 7, 1), 1, 254)
    scaled = (w * np.exp2(127.0 - byte)[:, None, :]).reshape(k, n).astype(np.float32)
    words = np.ascontiguousarray(scaled.reshape(k // 512, 128, 4, n).transpose(0, 1, 3, 2)).astype(ml_dtypes.float8_e4m3fn).view(np.uint8)
    return words, np.ascontiguousarray(byte.astype(np.uint8).reshape(k // 512, 16, n))


def unpack_weight(words, scales):
    g, p, n, _ = words.shape
    vals = np.ascontiguousarray(words).view(ml_dtypes.float8_e4m3fn).astype(np.float64) * np.repeat(np.exp2(scales.astype(np.float64) - 127.0), 8, axis=1)[..., None]
    return vals.transpose(0, 1, 3, 2).reshape(g * 512, n)


K, T, S, G, H, W = 512, 1024, 256, 2048, 512, 128


def setup_inputs():
    n = np.random.standard_normal
    s = mx_kscale(K)[:, None]
    packed_xT = pack_weight(n((K, T)) * s)
    packed_dT = pack_weight(n((K, G)) / s)
    perm = np.random.permutation(S)
    perm2 = np.random.permutation(S)
    perm3 = np.random.permutation(S)
    return {
        "x_words": packed_xT[0],
        "x_scales": packed_xT[1],
        "d_words": packed_dT[0],
        "d_scales": packed_dT[1],
        "gs": (np.random.uniform(0.5, 1.5, (K, 1)) * s).astype(np.float32),
        "offs": striped8(np.random.randint(0, T, (8, S))),
        "k1": striped8(np.random.randint(0, G, (8, H))),
        "hz": striped8(np.random.randint(0, T, (8, S))),
        "k2": striped8(np.random.randint(0, G, (8, H))),
        "n1": striped(perm[:W]),
        "n2": striped(perm[W:]),
        "n3": striped(np.random.permutation(S)),
        "k3": striped8(np.random.randint(0, G, (8, H))),
        "k4": striped8(np.random.randint(0, G, (8, H))),
        "two": striped(np.random.permutation(T)[:S]),
        "k5": striped8(np.random.randint(0, G, (8, H))),
        "hy": striped8(np.random.randint(0, T, (8, S))),
        "n4": striped(perm2[:W]),
        "n5": striped(perm2[W:]),
        "n6": striped(perm3[:W]),
        "n7": striped(perm3[W:]),
    }


def reference(x_words, x_scales, d_words, d_scales, gs, offs, k1, hz, k2, n1, n2, n3, k3, k4, two, k5, hy, n4, n5, n6, n7):
    d_k3 = unpack_weight(d_words, d_scales)[np.arange(K)[:, None], runs(k3, K)]
    d_k1 = unpack_weight(d_words, d_scales)[np.arange(K)[:, None], runs(k1, K)]
    xq = unpack_weight(x_words, x_scales)[np.arange(K)[:, None], runs(offs, K)]
    d_k2 = unpack_weight(d_words, d_scales)[np.arange(K)[:, None], runs(k2, K)]
    x_hz = unpack_weight(x_words, x_scales)[np.arange(K)[:, None], runs(hz, K)]
    h = 0.0625 * (d_k1.T @ xq + d_k2.T @ x_hz)
    pa = h[:, unstriped(n1)]
    pb = h[:, unstriped(n2)]
    rb = pa - pb
    ua = np.zeros((H, S))
    ua[:, unstriped(n1)] = pb
    ub = ua.copy()
    ub[:, unstriped(n2)] = rb
    z = f64(gs) * (np.maximum(ub, 0.5 * ub[:, unstriped(n3)]))
    d_k4 = unpack_weight(d_words, d_scales)[np.arange(K)[:, None], runs(k4, K)]
    x_two = unpack_weight(x_words, x_scales)[:, unstriped(two)]
    d_k5 = unpack_weight(d_words, d_scales)[np.arange(K)[:, None], runs(k5, K)]
    x_hy = unpack_weight(x_words, x_scales)[np.arange(K)[:, None], runs(hy, K)]
    h2 = 0.0625 * ((d_k3.T @ mxq(z, 0, "e4m3") + d_k4.T @ x_two + d_k5.T @ x_hy))
    pa2 = h2[:, unstriped(n4)]
    pb2 = h2[:, unstriped(n5)]
    rb2 = np.minimum(pa2, pb2)
    ra = np.maximum(pa2, pb2)
    ua2 = np.zeros((H, S))
    ua2[:, unstriped(n6)] = ra
    ub2 = ua2.copy()
    ub2[:, unstriped(n7)] = rb2
    return ub2 - h2

@@ -1,0 +1,220 @@
+from contextlib import ExitStack
+
+import concourse.mybir as mybir
+
+F32 = mybir.dt.float32
+BF16 = mybir.dt.bfloat16
+I32 = mybir.dt.int32
+U32 = mybir.dt.uint32
+U16 = mybir.dt.uint16
+U8 = mybir.dt.uint8
+FP8X4 = mybir.dt.float8_e4m3fn_x4
+ALU = mybir.AluOpType
+COPY = mybir.ActivationFunctionType.Copy
+
+P = 128
+PACK = 4
+K, T, S, G, H, W = 512, 1024, 256, 2048, 512, 128
+STRIPE = 16
+ROWS = 16
+FLOPS = 5 * 2 * K * H * S
+
+
+def tile_picked_mhhzmthswapdcpor_none_p_kernel(
+    tc, x_words, x_scales, d_words, d_scales, gs, offs, k1, hz, k2, n1, n2, n3, k3, k4, two, k5, hy, n4, n5, n6, n7, out
+):
+    nc = tc.nc
+    with ExitStack() as ctx:
+        held = ctx.enter_context(tc.tile_pool(name="held", bufs=1))
+        psum = ctx.enter_context(tc.psum_pool(name="psum", bufs=1))
+
+        lists = {}
+
+        def load_list(name, src):
+            lists[name] = held.tile([P, src.shape[1]], U16, name="list_" + name)
+            nc.sync.dma_start(lists[name][:], src)
+
+        def load_scales(name, src, width):
+            table = held.tile([P, width], U8, name=name, align_bytes=64)
+            rows = src[0].bitcast(I32)
+            nc.sync.dma_start(table[:].bitcast(I32), rows.unsqueeze(1).broadcast_to([ROWS, P // ROWS, width // 4]))
+            return table
+
+        def load_words(name, src, width):
+            table = held.tile([P, width], U32, name=name, align_bytes=64)
+            nc.sync.dma_start(table[:].bitcast(I32), src[0].rearrange("p n r -> p (n r)").bitcast(I32))
+            return table
+
+        x_bytes = load_scales("x_bytes", x_scales, T)
+        load_list("offs", offs)
+        load_list("hz", hz)
+        d_bytes = load_scales("d_bytes", d_scales, G)
+        load_list("k1", k1)
+        load_list("k2", k2)
+        x_table = load_words("x_table", x_words, T)
+        load_list("n1", n1)
+        d_table = load_words("d_table", d_words, G)
+        for name, src in (("n2", n2), ("n3", n3), ("two", two), ("hy", hy), ("k3", k3), ("k4", k4), ("k5", k5),
+                          ("n4", n4), ("n5", n5), ("n6", n6), ("n7", n7)):
+            load_list(name, src)
+        gain = held.tile([P, PACK], F32, name="gain")
+        nc.gpsimd.dma_start(gain[:], gs.rearrange("(p t) o -> p (t o)", t=PACK))
+
+        def entries(name, first, count):
+            return lists[name][:, first // STRIPE : (first + count) // STRIPE]
+
+        def gather(dst, table, offsets):
+            nc.vector.tensor_copy(dst, table[:].indirect(offsets))
+
+        def zeroed_plane(name, width):
+            plane = held.tile([P, width], U8, name=name, align_bytes=64)
+            nc.vector.memset(plane[:].bitcast(I32), 0)
+            return plane
+
+        def place_rows(plane, picked, queues):
+            for r in range(4):
+                queues[r % len(queues)].dma_start(plane[r:P:32, :].bitcast(I32), picked[8 * r : P : 32, :].bitcast(I32))
+
+        plane1 = zeroed_plane("plane1", 2 * H + 2 * S)
+        plane_x = zeroed_plane("plane_x", 2 * S)
+        plane_d = zeroed_plane("plane_d", 3 * H)
+
+        picked1 = held.tile([P, 2 * H + 2 * S], U8, name="picked1", align_bytes=64)
+        gather(picked1[:, 2 * H : 2 * H + S], x_bytes, lists["offs"][:])
+        gather(picked1[:, 2 * H + S :], x_bytes, lists["hz"][:])
+        gather(picked1[:, 0:H], d_bytes, lists["k1"][:])
+        gather(picked1[:, H : 2 * H], d_bytes, lists["k2"][:])
+        place_rows(plane1, picked1, (nc.sync, nc.scalar))
+
+        x_first = []
+        for name in ("offs", "hz"):
+            words = held.tile([P, S], U32, name="words_" + name, align_bytes=64)
+            gather(words[:], x_table, lists[name][:])
+            x_first.append(words)
+        picked_words = held.tile([P, 2 * H], U32, name="picked_words", align_bytes=64)
+        dealt_words = held.tile([P, PACK, 2, P], U32, name="dealt_words", align_bytes=64)
+        dealt_bytes = held.tile([P, PACK, 2, P], U8, name="dealt_bytes", align_bytes=64)
+        undealt_words = picked_words[:].rearrange("p (a m t) -> p t a m", a=2, t=PACK)
+        undealt_bytes = plane1[:, 0 : 2 * H].rearrange("p (a m t) -> p t a m", a=2, t=PACK)
+        for a, name in enumerate(("k1", "k2")):
+            gather(picked_words[:, a * H : (a + 1) * H], d_table, lists[name][:])
+        nc.vector.tensor_copy(dealt_bytes[:, 0], undealt_bytes[:, 0])
+        for a in range(2):
+            nc.vector.tensor_copy(dealt_words[:, 0, a], undealt_words[:, 0, a])
+        for dealt, undealt in ((dealt_bytes, undealt_bytes), (dealt_words, undealt_words)):
+            nc.vector.tensor_copy(dealt[:, 1:].rearrange("p t a m -> p a m t"), undealt[:, 1:].rearrange("p t a m -> p a m t"))
+
+        banks1 = [psum.tile([P, S], F32, name="bank1_%d" % t) for t in range(PACK)]
+        for t in range(PACK):
+            for a in range(2):
+                nc.tensor.matmul_mx(
+                    out=banks1[t][:],
+                    lhsT=dealt_words[:, t, a, :].bitcast(FP8X4),
+                    lhsT_scale=dealt_bytes[:, t, a, :],
+                    rhs=x_first[a][:].bitcast(FP8X4),
+                    rhs_scale=plane1[:, 2 * H + a * S : 2 * H + (a + 1) * S],
+                    start=(a == 0),
+                    stop=(a == 1),
+                )
+
+        second = {}
+
+        def second_bytes(names, table, plane, count, tag):
+            picked = held.tile([P, len(names) * count], U8, name="picked_" + names[0], tag=tag, align_bytes=64)
+            for a, name in enumerate(names):
+                for first in range(0, count, S):
+                    gather(picked[:, a * count + first : a * count + first + S], table, entries(name, first, S))
+            place_rows(plane, picked, (nc.sync,))
+
+        def second_words(name, table, half, tag):
+            words = held.tile([P, S], U32, name="words_%s_%d" % (name, half), tag=tag, align_bytes=64)
+            gather(words[:], table, entries(name, half * S, S))
+            second[name, half] = words
+
+        z = held.tile([P, S * PACK], BF16, name="z", align_bytes=64)
+        z_words = held.tile([P, S], U32, name="z_words", align_bytes=64)
+        z_bytes = held.tile([P, S], U8, name="z_bytes", align_bytes=64)
+
+        def first_step(t):
+            h = held.tile([P, S], F32, name="h_%d" % t, align_bytes=64)
+            if t == 0:
+                nc.scalar.activation(h[:], banks1[t][:], COPY, scale=0.0625)
+            else:
+                nc.vector.tensor_scalar_mul(h[:], banks1[t][:], 0.0625)
+            pa = held.tile([P, W], F32, name="pa_%d" % t, align_bytes=64)
+            pb = held.tile([P, W], F32, name="pb_%d" % t, align_bytes=64)
+            rb = held.tile([P, W], F32, name="rb_%d" % t, align_bytes=64)
+            ub = held.tile([P, S], F32, name="ub_%d" % t, align_bytes=64)
+            nc.scalar.activation(pa[:], h[:].indirect(lists["n1"][:]), COPY)
+            nc.scalar.activation(pb[:], h[:].indirect(lists["n2"][:]), COPY)
+            nc.vector.tensor_sub(rb[:], pa[:], pb[:])
+            nc.scalar.activation(ub[:].indirect(lists["n1"][:]), pb[:], COPY)
+            nc.scalar.activation(ub[:].indirect(lists["n2"][:]), rb[:], COPY)
+            other = held.tile([P, S], F32, name="other_%d" % t, align_bytes=64)
+            larger = held.tile([P, S], F32, name="larger_%d" % t, align_bytes=64)
+            for half in range(2):
+                cols = slice(half * W, (half + 1) * W)
+                nc.scalar.activation(other[:, cols], ub[:].indirect(entries("n3", half * W, W)), COPY)
+                nc.vector.scalar_tensor_tensor(larger[:, cols], other[:, cols], 0.5, ub[:, cols], ALU.mult, ALU.max)
+                nc.vector.tensor_scalar_mul(
+                    z[:, half * W * PACK + t : (half + 1) * W * PACK : PACK], larger[:, cols], gain[:, t : t + 1]
+                )
+
+        second_bytes(("two", "hy"), x_bytes, plane_x, S, "picked_words")
+        first_step(0)
+        second_bytes(("k3", "k4", "k5"), d_bytes, plane_d, H, "pa_0")
+        first_step(1)
+        second_words("two", x_table, 0, "pa_1")
+        first_step(2)
+        second_words("hy", x_table, 0, "larger_0")
+        second_words("k4", d_table, 0, "pa_2")
+        second_words("k5", d_table, 0, "larger_1")
+        first_step(3)
+        second_words("k3", d_table, 0, "pa_3")
+        for half in range(2):
+            cols = slice(half * W, (half + 1) * W)
+            nc.vector.quantize_mx(
+                out=z_words[:, cols].bitcast(FP8X4), scales=z_bytes[:, cols], in_=z[:, half * W * PACK : (half + 1) * W * PACK]
+            )
+        second_words("k4", d_table, 1, "z")
+        second_words("k5", d_table, 1, "larger_3")
+        second_words("k3", d_table, 1, "other_3")
+
+        for u in range(H // P):
+            half, cols = u // 2, slice((u % 2) * P, (u % 2 + 1) * P)
+            bank = psum.tile([P, S], F32, name="bank2_%d" % u)
+
+            def stationary(a):
+                first = a * H + u * P
+                return dict(lhsT=second[("k3", "k4", "k5")[a], half][:, cols].bitcast(FP8X4), lhsT_scale=plane_d[:, first : first + P])
+
+            for a in range(2):
+                nc.tensor.matmul_mx(
+                    out=bank[:], rhs=second[("two", "hy")[a], 0][:].bitcast(FP8X4), rhs_scale=plane_x[:, a * S : (a + 1) * S],
+                    start=(a == 0), stop=False, **stationary(1 + a)
+                )
+            for part in range(2):
+                places = slice(part * W, (part + 1) * W)
+                nc.tensor.matmul_mx(
+                    out=bank[:, places], rhs=z_words[:, places].bitcast(FP8X4), rhs_scale=z_bytes[:, places],
+                    start=False, stop=(part == 1), **stationary(0)
+                )
+            h2 = held.tile([P, S], F32, name="h2_%d" % u, align_bytes=64)
+            if u == 0:
+                nc.scalar.activation(h2[:], bank[:], COPY, scale=0.0625)
+            else:
+                nc.vector.tensor_scalar_mul(h2[:], bank[:], 0.0625)
+            pa2 = held.tile([P, W], F32, name="pa2_%d" % u, align_bytes=64)
+            pb2 = held.tile([P, W], F32, name="pb2_%d" % u, align_bytes=64)
+            ra = held.tile([P, W], F32, name="ra_%d" % u, align_bytes=64)
+            rb2 = held.tile([P, W], F32, name="rb2_%d" % u, align_bytes=64)
+            ub2 = held.tile([P, S], F32, name="ub2_%d" % u, align_bytes=64)
+            result = held.tile([P, S], F32, name="result_%d" % u, align_bytes=64)
+            nc.scalar.activation(pa2[:], h2[:].indirect(lists["n4"][:]), COPY)
+            nc.scalar.activation(pb2[:], h2[:].indirect(lists["n5"][:]), COPY)
+            nc.vector.tensor_tensor(ra[:], pa2[:], pb2[:], ALU.max)
+            nc.vector.tensor_tensor(rb2[:], pa2[:], pb2[:], ALU.min)
+            nc.scalar.activation(ub2[:].indirect(lists["n6"][:]), ra[:], COPY)
+            nc.scalar.activation(ub2[:].indirect(lists["n7"][:]), rb2[:], COPY)
+            nc.vector.tensor_sub(result[:], ub2[:], h2[:])
+            nc.sync.dma_start(out[u * P : (u + 1) * P, :], result[:])

@@ -58,7 +58,7 @@ def tile_picked_mhhzmthswapdcpor_none_p_kernel(
                           ("n4", n4), ("n5", n5), ("n6", n6), ("n7", n7)):
             load_list(name, src)
         gain = held.tile([P, PACK], F32, name="gain")
-        nc.gpsimd.dma_start(gain[:], gs.rearrange("(p t) o -> p (t o)", t=PACK))
+        nc.scalar.dma_start(gain[:], gs.rearrange("(p t) o -> p (t o)", t=PACK))
 
         def entries(name, first, count):
             return lists[name][:, first // STRIPE : (first + count) // STRIPE]
@@ -72,19 +72,23 @@ def tile_picked_mhhzmthswapdcpor_none_p_kernel(
             return plane
 
         def place_rows(plane, picked, queues):
-            for r in range(4):
-                queues[r % len(queues)].dma_start(plane[r:P:32, :].bitcast(I32), picked[8 * r : P : 32, :].bitcast(I32))
+            for q in range(4):
+                queues[q % len(queues)].dma_start(
+                    plane[32 * q : 32 * q + 4, :].bitcast(I32), picked[32 * q : 32 * (q + 1) : 8, :].bitcast(I32)
+                )
 
         plane1 = zeroed_plane("plane1", 2 * H + 2 * S)
-        plane_x = zeroed_plane("plane_x", 2 * S)
-        plane_d = zeroed_plane("plane_d", 3 * H)
+        plane2 = zeroed_plane("plane2", 2 * S + 3 * H)
 
+        ub = [held.tile([P, S + STRIPE], F32, name="ub_%d" % t, align_bytes=64) for t in range(PACK)]
+        for t in range(PACK):
+            nc.vector.memset(ub[t][:, S:], 0.0)
         picked1 = held.tile([P, 2 * H + 2 * S], U8, name="picked1", align_bytes=64)
         gather(picked1[:, 2 * H : 2 * H + S], x_bytes, lists["offs"][:])
         gather(picked1[:, 2 * H + S :], x_bytes, lists["hz"][:])
         gather(picked1[:, 0:H], d_bytes, lists["k1"][:])
         gather(picked1[:, H : 2 * H], d_bytes, lists["k2"][:])
-        place_rows(plane1, picked1, (nc.sync, nc.scalar))
+        place_rows(plane1, picked1, (nc.sync,))
 
         x_first = []
         for name in ("offs", "hz"):
@@ -92,7 +96,8 @@ def tile_picked_mhhzmthswapdcpor_none_p_kernel(
             gather(words[:], x_table, lists[name][:])
             x_first.append(words)
         picked_words = held.tile([P, 2 * H], U32, name="picked_words", align_bytes=64)
-        dealt_words = held.tile([P, PACK, 2, P], U32, name="dealt_words", align_bytes=64)
+        first_words = held.tile([P, 2, P], U32, name="first_words", align_bytes=64)
+        later_words = held.tile([P, PACK - 1, 2, P], U32, name="later_words", tag="picked1", align_bytes=64)
         dealt_bytes = held.tile([P, PACK, 2, P], U8, name="dealt_bytes", align_bytes=64)
         undealt_words = picked_words[:].rearrange("p (a m t) -> p t a m", a=2, t=PACK)
         undealt_bytes = plane1[:, 0 : 2 * H].rearrange("p (a m t) -> p t a m", a=2, t=PACK)
@@ -100,16 +105,16 @@ def tile_picked_mhhzmthswapdcpor_none_p_kernel(
             gather(picked_words[:, a * H : (a + 1) * H], d_table, lists[name][:])
         nc.vector.tensor_copy(dealt_bytes[:, 0], undealt_bytes[:, 0])
         for a in range(2):
-            nc.vector.tensor_copy(dealt_words[:, 0, a], undealt_words[:, 0, a])
-        for dealt, undealt in ((dealt_bytes, undealt_bytes), (dealt_words, undealt_words)):
-            nc.vector.tensor_copy(dealt[:, 1:].rearrange("p t a m -> p a m t"), undealt[:, 1:].rearrange("p t a m -> p a m t"))
+            nc.vector.tensor_copy(first_words[:, a], undealt_words[:, 0, a])
+        for dealt, undealt in ((dealt_bytes[:, 1:], undealt_bytes), (later_words[:], undealt_words)):
+            nc.vector.tensor_copy(dealt.rearrange("p t a m -> p a m t"), undealt[:, 1:].rearrange("p t a m -> p a m t"))
 
         banks1 = [psum.tile([P, S], F32, name="bank1_%d" % t) for t in range(PACK)]
         for t in range(PACK):
             for a in range(2):
                 nc.tensor.matmul_mx(
                     out=banks1[t][:],
-                    lhsT=dealt_words[:, t, a, :].bitcast(FP8X4),
+                    lhsT=(first_words[:, a, :] if t == 0 else later_words[:, t - 1, a, :]).bitcast(FP8X4),
                     lhsT_scale=dealt_bytes[:, t, a, :],
                     rhs=x_first[a][:].bitcast(FP8X4),
                     rhs_scale=plane1[:, 2 * H + a * S : 2 * H + (a + 1) * S],
@@ -118,103 +123,151 @@ def tile_picked_mhhzmthswapdcpor_none_p_kernel(
                 )
 
         second = {}
+        scale_rows = {}
 
-        def second_bytes(names, table, plane, count, tag):
-            picked = held.tile([P, len(names) * count], U8, name="picked_" + names[0], tag=tag, align_bytes=64)
-            for a, name in enumerate(names):
-                for first in range(0, count, S):
-                    gather(picked[:, a * count + first : a * count + first + S], table, entries(name, first, S))
-            place_rows(plane, picked, (nc.sync,))
+        def second_bytes(tag):
+            picked = held.tile([P, 2 * S + 3 * H], U8, name="picked2", tag=tag, align_bytes=64)
+            first = 0
+            for name, table, count in (("two", x_bytes, S), ("hy", x_bytes, S), ("k4", d_bytes, H), ("k5", d_bytes, H), ("k3", d_bytes, H)):
+                gather(picked[:, first : first + count], table, lists[name][:])
+                scale_rows[name] = plane2[:, first : first + count]
+                first = first + count
+            place_rows(plane2, picked, (nc.sync,))
 
-        def second_words(name, table, half, tag):
-            words = held.tile([P, S], U32, name="words_%s_%d" % (name, half), tag=tag, align_bytes=64)
-            gather(words[:], table, entries(name, half * S, S))
-            second[name, half] = words
+        def second_words(pieces, table, tag):
+            words = held.tile([P, len(pieces) * S], U32, name="words_%s_%d" % pieces[0], tag=tag, align_bytes=64)
+            for a, (name, half) in enumerate(pieces):
+                second[name, half] = words[:, a * S : (a + 1) * S]
+                gather(second[name, half], table, entries(name, half * S, S))
 
         z = held.tile([P, S * PACK], BF16, name="z", align_bytes=64)
         z_words = held.tile([P, S], U32, name="z_words", align_bytes=64)
         z_bytes = held.tile([P, S], U8, name="z_bytes", align_bytes=64)
 
-        def first_step(t):
-            h = held.tile([P, S], F32, name="h_%d" % t, align_bytes=64)
-            if t == 0:
-                nc.scalar.activation(h[:], banks1[t][:], COPY, scale=0.0625)
+        def floats(name, width, tag=None):
+            return held.tile([P, width], F32, name=name, tag=tag or name, align_bytes=64)
+
+        def leave_bank(name, bank, on_scalar):
+            tile = floats(name, S)
+            if on_scalar:
+                nc.scalar.activation(tile[:], bank[:], COPY, scale=0.0625)
             else:
-                nc.vector.tensor_scalar_mul(h[:], banks1[t][:], 0.0625)
-            pa = held.tile([P, W], F32, name="pa_%d" % t, align_bytes=64)
-            pb = held.tile([P, W], F32, name="pb_%d" % t, align_bytes=64)
-            rb = held.tile([P, W], F32, name="rb_%d" % t, align_bytes=64)
-            ub = held.tile([P, S], F32, name="ub_%d" % t, align_bytes=64)
-            nc.scalar.activation(pa[:], h[:].indirect(lists["n1"][:]), COPY)
-            nc.scalar.activation(pb[:], h[:].indirect(lists["n2"][:]), COPY)
-            nc.vector.tensor_sub(rb[:], pa[:], pb[:])
-            nc.scalar.activation(ub[:].indirect(lists["n1"][:]), pb[:], COPY)
-            nc.scalar.activation(ub[:].indirect(lists["n2"][:]), rb[:], COPY)
-            other = held.tile([P, S], F32, name="other_%d" % t, align_bytes=64)
-            larger = held.tile([P, S], F32, name="larger_%d" % t, align_bytes=64)
-            for half in range(2):
-                cols = slice(half * W, (half + 1) * W)
-                nc.scalar.activation(other[:, cols], ub[:].indirect(entries("n3", half * W, W)), COPY)
-                nc.vector.scalar_tensor_tensor(larger[:, cols], other[:, cols], 0.5, ub[:, cols], ALU.mult, ALU.max)
+                nc.vector.tensor_scalar_mul(tile[:], bank[:], 0.0625)
+            return tile
+
+        def fetch(dst, window, offsets):
+            nc.scalar.activation(dst, window[:].indirect(offsets), COPY)
+
+        def put(window, name, values):
+            nc.scalar.activation(window[:].indirect(lists[name][:]), values, COPY)
+
+        h = {}
+        pb, rb = {}, {}
+
+        def pair_up(t):
+            pa = floats("pa_%d" % t, W)
+            pb[t] = floats("pb_%d" % t, W)
+            rb[t] = floats("rb_%d" % t, W, tag="picked1" if t == 0 else None)
+            fetch(pb[t][:], h[t], lists["n2"][:])
+            fetch(pa[:], h[t], lists["n1"][:])
+            nc.vector.tensor_sub(rb[t][:], pa[:], pb[t][:])
+
+        def put_pb(t):
+            put(ub[t], "n1", pb[t][:])
+
+        def put_rb(t):
+            put(ub[t], "n2", rb[t][:])
+
+        def make_z(t):
+            other = floats("other_%d" % t, S)
+            larger = floats("larger_%d" % t, S)
+            width = W if t == PACK - 1 else S
+            for first in range(0, S, width):
+                cols = slice(first, first + width)
+                fetch(other[:, cols], ub[t], entries("n3", first, width))
+                nc.vector.scalar_tensor_tensor(larger[:, cols], other[:, cols], 0.5, ub[t][:, cols], ALU.mult, ALU.max)
                 nc.vector.tensor_scalar_mul(
-                    z[:, half * W * PACK + t : (half + 1) * W * PACK : PACK], larger[:, cols], gain[:, t : t + 1]
+                    z[:, first * PACK + t : (first + width) * PACK : PACK], larger[:, cols], gain[:, t : t + 1]
                 )
 
-        second_bytes(("two", "hy"), x_bytes, plane_x, S, "picked_words")
-        first_step(0)
-        second_bytes(("k3", "k4", "k5"), d_bytes, plane_d, H, "pa_0")
-        first_step(1)
-        second_words("two", x_table, 0, "pa_1")
-        first_step(2)
-        second_words("hy", x_table, 0, "larger_0")
-        second_words("k4", d_table, 0, "pa_2")
-        second_words("k5", d_table, 0, "larger_1")
-        first_step(3)
-        second_words("k3", d_table, 0, "pa_3")
+        h[0] = leave_bank("h_0", banks1[0], True)
+        pair_up(0)
+        put_pb(0)
+        for t in range(1, PACK):
+            h[t] = leave_bank("h_%d" % t, banks1[t], True)
+        for t in range(1, PACK):
+            pair_up(t)
+        second_words((("two", 0), ("hy", 0)), x_table, "picked_words")
+        second_bytes("pa_0")
+        second_words((("k4", 0), ("k5", 0), ("k3", 0)), d_table, "pa_2")
+        put_rb(0)
+        put_pb(1)
+        make_z(0)
+        put_pb(2)
+        put_rb(1)
+        put_pb(3)
+        put_rb(2)
+        make_z(1)
+        make_z(2)
+        put_rb(3)
+        make_z(3)
         for half in range(2):
             cols = slice(half * W, (half + 1) * W)
             nc.vector.quantize_mx(
                 out=z_words[:, cols].bitcast(FP8X4), scales=z_bytes[:, cols], in_=z[:, half * W * PACK : (half + 1) * W * PACK]
             )
-        second_words("k4", d_table, 1, "z")
-        second_words("k5", d_table, 1, "larger_3")
-        second_words("k3", d_table, 1, "other_3")
+        second_words((("k4", 1), ("k5", 1), ("k3", 1)), d_table, "z")
 
-        for u in range(H // P):
+        h2, ra, rb2, ub2 = {}, {}, {}, {}
+
+        def second_product(u):
             half, cols = u // 2, slice((u % 2) * P, (u % 2 + 1) * P)
             bank = psum.tile([P, S], F32, name="bank2_%d" % u)
 
-            def stationary(a):
-                first = a * H + u * P
-                return dict(lhsT=second[("k3", "k4", "k5")[a], half][:, cols].bitcast(FP8X4), lhsT_scale=plane_d[:, first : first + P])
+            def stationary(name):
+                return dict(lhsT=second[name, half][:, cols].bitcast(FP8X4), lhsT_scale=scale_rows[name][:, u * P : (u + 1) * P])
 
-            for a in range(2):
+            for coded, moving in (("k4", "two"), ("k5", "hy")):
                 nc.tensor.matmul_mx(
-                    out=bank[:], rhs=second[("two", "hy")[a], 0][:].bitcast(FP8X4), rhs_scale=plane_x[:, a * S : (a + 1) * S],
-                    start=(a == 0), stop=False, **stationary(1 + a)
+                    out=bank[:], rhs=second[moving, 0].bitcast(FP8X4), rhs_scale=scale_rows[moving],
+                    start=(coded == "k4"), stop=False, **stationary(coded)
                 )
             for part in range(2):
                 places = slice(part * W, (part + 1) * W)
                 nc.tensor.matmul_mx(
                     out=bank[:, places], rhs=z_words[:, places].bitcast(FP8X4), rhs_scale=z_bytes[:, places],
-                    start=False, stop=(part == 1), **stationary(0)
+                    start=False, stop=(part == 1), **stationary("k3")
                 )
-            h2 = held.tile([P, S], F32, name="h2_%d" % u, align_bytes=64)
-            if u == 0:
-                nc.scalar.activation(h2[:], bank[:], COPY, scale=0.0625)
-            else:
-                nc.vector.tensor_scalar_mul(h2[:], bank[:], 0.0625)
-            pa2 = held.tile([P, W], F32, name="pa2_%d" % u, align_bytes=64)
-            pb2 = held.tile([P, W], F32, name="pb2_%d" % u, align_bytes=64)
-            ra = held.tile([P, W], F32, name="ra_%d" % u, align_bytes=64)
-            rb2 = held.tile([P, W], F32, name="rb2_%d" % u, align_bytes=64)
-            ub2 = held.tile([P, S], F32, name="ub2_%d" % u, align_bytes=64)
-            result = held.tile([P, S], F32, name="result_%d" % u, align_bytes=64)
-            nc.scalar.activation(pa2[:], h2[:].indirect(lists["n4"][:]), COPY)
-            nc.scalar.activation(pb2[:], h2[:].indirect(lists["n5"][:]), COPY)
-            nc.vector.tensor_tensor(ra[:], pa2[:], pb2[:], ALU.max)
-            nc.vector.tensor_tensor(rb2[:], pa2[:], pb2[:], ALU.min)
-            nc.scalar.activation(ub2[:].indirect(lists["n6"][:]), ra[:], COPY)
-            nc.scalar.activation(ub2[:].indirect(lists["n7"][:]), rb2[:], COPY)
-            nc.vector.tensor_sub(result[:], ub2[:], h2[:])
+            h2[u] = leave_bank("h2_%d" % u, bank, u < 2)
+
+        def pair_up2(u):
+            pa2 = floats("pa2_%d" % u, W)
+            pb2 = floats("pb2_%d" % u, W)
+            ra[u] = floats("ra_%d" % u, W)
+            rb2[u] = floats("rb2_%d" % u, W)
+            ub2[u] = floats("ub2_%d" % u, S)
+            fetch(pa2[:], h2[u], lists["n4"][:])
+            fetch(pb2[:], h2[u], lists["n5"][:])
+            nc.vector.tensor_tensor(ra[u][:], pa2[:], pb2[:], ALU.max)
+            nc.vector.tensor_tensor(rb2[u][:], pa2[:], pb2[:], ALU.min)
+
+        def finish(u):
+            put(ub2[u], "n7", rb2[u][:])
+            result = floats("result_%d" % u, S)
+            nc.vector.tensor_sub(result[:], ub2[u][:], h2[u][:])
             nc.sync.dma_start(out[u * P : (u + 1) * P, :], result[:])
+
+        second_product(0)
+        second_product(1)
+        pair_up2(0)
+        pair_up2(1)
+        second_product(2)
+        second_product(3)
+        for first in (0, 2):
+            if first:
+                pair_up2(first)
+                pair_up2(first + 1)
+            put(ub2[first], "n6", ra[first][:])
+            put(ub2[first + 1], "n6", ra[first + 1][:])
+            finish(first)
+            finish(first + 1)

@@ -96,8 +96,7 @@ def tile_picked_mhhzmthswapdcpor_none_p_kernel(
             gather(words[:], x_table, lists[name][:])
             x_first.append(words)
         picked_words = held.tile([P, 2 * H], U32, name="picked_words", align_bytes=64)
-        first_words = held.tile([P, 2, P], U32, name="first_words", align_bytes=64)
-        later_words = held.tile([P, PACK - 1, 2, P], U32, name="later_words", tag="picked1", align_bytes=64)
+        dealt_words = held.tile([P, PACK, 2, P], U32, name="dealt_words", tag="picked1", align_bytes=64)
         dealt_bytes = held.tile([P, PACK, 2, P], U8, name="dealt_bytes", align_bytes=64)
         undealt_words = picked_words[:].rearrange("p (a m t) -> p t a m", a=2, t=PACK)
         undealt_bytes = plane1[:, 0 : 2 * H].rearrange("p (a m t) -> p t a m", a=2, t=PACK)
@@ -105,8 +104,8 @@ def tile_picked_mhhzmthswapdcpor_none_p_kernel(
             gather(picked_words[:, a * H : (a + 1) * H], d_table, lists[name][:])
         nc.vector.tensor_copy(dealt_bytes[:, 0], undealt_bytes[:, 0])
         for a in range(2):
-            nc.vector.tensor_copy(first_words[:, a], undealt_words[:, 0, a])
-        for dealt, undealt in ((dealt_bytes[:, 1:], undealt_bytes), (later_words[:], undealt_words)):
+            nc.vector.tensor_copy(dealt_words[:, 0, a], undealt_words[:, 0, a])
+        for dealt, undealt in ((dealt_bytes[:, 1:], undealt_bytes), (dealt_words[:, 1:], undealt_words)):
             nc.vector.tensor_copy(dealt.rearrange("p t a m -> p a m t"), undealt[:, 1:].rearrange("p t a m -> p a m t"))
 
         banks1 = [psum.tile([P, S], F32, name="bank1_%d" % t) for t in range(PACK)]
@@ -114,7 +113,7 @@ def tile_picked_mhhzmthswapdcpor_none_p_kernel(
             for a in range(2):
                 nc.tensor.matmul_mx(
                     out=banks1[t][:],
-                    lhsT=(first_words[:, a, :] if t == 0 else later_words[:, t - 1, a, :]).bitcast(FP8X4),
+                    lhsT=dealt_words[:, t, a, :].bitcast(FP8X4),
                     lhsT_scale=dealt_bytes[:, t, a, :],
                     rhs=x_first[a][:].bitcast(FP8X4),
                     rhs_scale=plane1[:, 2 * H + a * S : 2 * H + (a + 1) * S],
@@ -170,7 +169,7 @@ def tile_picked_mhhzmthswapdcpor_none_p_kernel(
             rb[t] = floats("rb_%d" % t, W, tag="picked1" if t == 0 else None)
             fetch(pb[t][:], h[t], lists["n2"][:])
             fetch(pa[:], h[t], lists["n1"][:])
-            nc.vector.tensor_sub(rb[t][:], pa[:], pb[t][:])
+            nc.gpsimd.tensor_sub(rb[t][:], pa[:], pb[t][:])
 
         def put_pb(t):
             put(ub[t], "n1", pb[t][:])
@@ -194,12 +193,12 @@ def tile_picked_mhhzmthswapdcpor_none_p_kernel(
         pair_up(0)
         put_pb(0)
         for t in range(1, PACK):
-            h[t] = leave_bank("h_%d" % t, banks1[t], True)
+            h[t] = leave_bank("h_%d" % t, banks1[t], t == 1)
         for t in range(1, PACK):
             pair_up(t)
         second_words((("two", 0), ("hy", 0)), x_table, "picked_words")
-        second_bytes("pa_0")
-        second_words((("k4", 0), ("k5", 0), ("k3", 0)), d_table, "pa_2")
+        second_bytes("words_offs")
+        second_words((("k4", 0), ("k5", 0), ("k3", 0)), d_table, "words_hz")
         put_rb(0)
         put_pb(1)
         make_z(0)

@@ -58,7 +58,7 @@ def tile_picked_mhhzmthswapdcpor_none_p_kernel(
                           ("n4", n4), ("n5", n5), ("n6", n6), ("n7", n7)):
             load_list(name, src)
         gain = held.tile([P, PACK], F32, name="gain")
-        nc.scalar.dma_start(gain[:], gs.rearrange("(p t) o -> p (t o)", t=PACK))
+        nc.gpsimd.dma_start(gain[:], gs.rearrange("(p t) o -> p (t o)", t=PACK))
 
         def entries(name, first, count):
             return lists[name][:, first // STRIPE : (first + count) // STRIPE]
@@ -88,7 +88,7 @@ def tile_picked_mhhzmthswapdcpor_none_p_kernel(
         gather(picked1[:, 2 * H + S :], x_bytes, lists["hz"][:])
         gather(picked1[:, 0:H], d_bytes, lists["k1"][:])
         gather(picked1[:, H : 2 * H], d_bytes, lists["k2"][:])
-        place_rows(plane1, picked1, (nc.sync,))
+        place_rows(plane1, picked1, (nc.scalar,))
 
         x_first = []
         for name in ("offs", "hz"):

from contextlib import ExitStack

import concourse.mybir as mybir

F32 = mybir.dt.float32
BF16 = mybir.dt.bfloat16
I32 = mybir.dt.int32
U32 = mybir.dt.uint32
U16 = mybir.dt.uint16
U8 = mybir.dt.uint8
FP8X4 = mybir.dt.float8_e4m3fn_x4
ALU = mybir.AluOpType
COPY = mybir.ActivationFunctionType.Copy

P = 128
PACK = 4
K, T, S, G, H, W = 512, 1024, 256, 2048, 512, 128
STRIPE = 16
ROWS = 16
FLOPS = 5 * 2 * K * H * S


def tile_picked_mhhzmthswapdcpor_none_p_kernel(
    tc, x_words, x_scales, d_words, d_scales, gs, offs, k1, hz, k2, n1, n2, n3, k3, k4, two, k5, hy, n4, n5, n6, n7, out
):
    nc = tc.nc
    with ExitStack() as ctx:
        held = ctx.enter_context(tc.tile_pool(name="held", bufs=1))
        psum = ctx.enter_context(tc.psum_pool(name="psum", bufs=1))

        lists = {}

        def load_list(name, src):
            lists[name] = held.tile([P, src.shape[1]], U16, name="list_" + name)
            nc.sync.dma_start(lists[name][:], src)

        def load_scales(name, src, width):
            table = held.tile([P, width], U8, name=name, align_bytes=64)
            rows = src[0].bitcast(I32)
            nc.sync.dma_start(table[:].bitcast(I32), rows.unsqueeze(1).broadcast_to([ROWS, P // ROWS, width // 4]))
            return table

        def load_words(name, src, width):
            table = held.tile([P, width], U32, name=name, align_bytes=64)
            nc.sync.dma_start(table[:].bitcast(I32), src[0].rearrange("p n r -> p (n r)").bitcast(I32))
            return table

        x_bytes = load_scales("x_bytes", x_scales, T)
        load_list("offs", offs)
        load_list("hz", hz)
        d_bytes = load_scales("d_bytes", d_scales, G)
        load_list("k1", k1)
        load_list("k2", k2)
        x_table = load_words("x_table", x_words, T)
        load_list("n1", n1)
        d_table = load_words("d_table", d_words, G)
        for name, src in (("n2", n2), ("n3", n3), ("two", two), ("hy", hy), ("k3", k3), ("k4", k4), ("k5", k5),
                          ("n4", n4), ("n5", n5), ("n6", n6), ("n7", n7)):
            load_list(name, src)
        gain = held.tile([P, PACK], F32, name="gain")
        nc.gpsimd.dma_start(gain[:], gs.rearrange("(p t) o -> p (t o)", t=PACK))

        def entries(name, first, count):
            return lists[name][:, first // STRIPE : (first + count) // STRIPE]

        def gather(dst, table, offsets):
            nc.vector.tensor_copy(dst, table[:].indirect(offsets))

        def zeroed_plane(name, width):
            plane = held.tile([P, width], U8, name=name, align_bytes=64)
            nc.vector.memset(plane[:].bitcast(I32), 0)
            return plane

        def place_rows(plane, picked, queues):
            for q in range(4):
                queues[q % len(queues)].dma_start(
                    plane[32 * q : 32 * q + 4, :].bitcast(I32), picked[32 * q : 32 * (q + 1) : 8, :].bitcast(I32)
                )

        plane1 = zeroed_plane("plane1", 2 * H + 2 * S)
        plane2 = zeroed_plane("plane2", 2 * S + 3 * H)

        ub = [held.tile([P, S + STRIPE], F32, name="ub_%d" % t, align_bytes=64) for t in range(PACK)]
        for t in range(PACK):
            nc.vector.memset(ub[t][:, S:], 0.0)
        picked1 = held.tile([P, 2 * H + 2 * S], U8, name="picked1", align_bytes=64)
        gather(picked1[:, 2 * H : 2 * H + S], x_bytes, lists["offs"][:])
        gather(picked1[:, 2 * H + S :], x_bytes, lists["hz"][:])
        gather(picked1[:, 0:H], d_bytes, lists["k1"][:])
        gather(picked1[:, H : 2 * H], d_bytes, lists["k2"][:])
        place_rows(plane1, picked1, (nc.scalar,))

        x_first = []
        for name in ("offs", "hz"):
            words = held.tile([P, S], U32, name="words_" + name, align_bytes=64)
            gather(words[:], x_table, lists[name][:])
            x_first.append(words)
        picked_words = held.tile([P, 2 * H], U32, name="picked_words", align_bytes=64)
        dealt_words = held.tile([P, PACK, 2, P], U32, name="dealt_words", tag="picked1", align_bytes=64)
        dealt_bytes = held.tile([P, PACK, 2, P], U8, name="dealt_bytes", align_bytes=64)
        undealt_words = picked_words[:].rearrange("p (a m t) -> p t a m", a=2, t=PACK)
        undealt_bytes = plane1[:, 0 : 2 * H].rearrange("p (a m t) -> p t a m", a=2, t=PACK)
        for a, name in enumerate(("k1", "k2")):
            gather(picked_words[:, a * H : (a + 1) * H], d_table, lists[name][:])
        nc.vector.tensor_copy(dealt_bytes[:, 0], undealt_bytes[:, 0])
        for a in range(2):
            nc.vector.tensor_copy(dealt_words[:, 0, a], undealt_words[:, 0, a])
        for dealt, undealt in ((dealt_bytes[:, 1:], undealt_bytes), (dealt_words[:, 1:], undealt_words)):
            nc.vector.tensor_copy(dealt.rearrange("p t a m -> p a m t"), undealt[:, 1:].rearrange("p t a m -> p a m t"))

        banks1 = [psum.tile([P, S], F32, name="bank1_%d" % t) for t in range(PACK)]
        for t in range(PACK):
            for a in range(2):
                nc.tensor.matmul_mx(
                    out=banks1[t][:],
                    lhsT=dealt_words[:, t, a, :].bitcast(FP8X4),
                    lhsT_scale=dealt_bytes[:, t, a, :],
                    rhs=x_first[a][:].bitcast(FP8X4),
                    rhs_scale=plane1[:, 2 * H + a * S : 2 * H + (a + 1) * S],
                    start=(a == 0),
                    stop=(a == 1),
                )

        second = {}
        scale_rows = {}

        def second_bytes(tag):
            picked = held.tile([P, 2 * S + 3 * H], U8, name="picked2", tag=tag, align_bytes=64)
            first = 0
            for name, table, count in (("two", x_bytes, S), ("hy", x_bytes, S), ("k4", d_bytes, H), ("k5", d_bytes, H), ("k3", d_bytes, H)):
                gather(picked[:, first : first + count], table, lists[name][:])
                scale_rows[name] = plane2[:, first : first + count]
                first = first + count
            place_rows(plane2, picked, (nc.sync,))

        def second_words(pieces, table, tag):
            words = held.tile([P, len(pieces) * S], U32, name="words_%s_%d" % pieces[0], tag=tag, align_bytes=64)
            for a, (name, half) in enumerate(pieces):
                second[name, half] = words[:, a * S : (a + 1) * S]
                gather(second[name, half], table, entries(name, half * S, S))

        z = held.tile([P, S * PACK], BF16, name="z", align_bytes=64)
        z_words = held.tile([P, S], U32, name="z_words", align_bytes=64)
        z_bytes = held.tile([P, S], U8, name="z_bytes", align_bytes=64)

        def floats(name, width, tag=None):
            return held.tile([P, width], F32, name=name, tag=tag or name, align_bytes=64)

        def leave_bank(name, bank, on_scalar):
            tile = floats(name, S)
            if on_scalar:
                nc.scalar.activation(tile[:], bank[:], COPY, scale=0.0625)
            else:
                nc.vector.tensor_scalar_mul(tile[:], bank[:], 0.0625)
            return tile

        def fetch(dst, window, offsets):
            nc.scalar.activation(dst, window[:].indirect(offsets), COPY)

        def put(window, name, values):
            nc.scalar.activation(window[:].indirect(lists[name][:]), values, COPY)

        h = {}
        pb, rb = {}, {}

        def pair_up(t):
            pa = floats("pa_%d" % t, W)
            pb[t] = floats("pb_%d" % t, W)
            rb[t] = floats("rb_%d" % t, W, tag="picked1" if t == 0 else None)
            fetch(pb[t][:], h[t], lists["n2"][:])
            fetch(pa[:], h[t], lists["n1"][:])
            nc.gpsimd.tensor_sub(rb[t][:], pa[:], pb[t][:])

        def put_pb(t):
            put(ub[t], "n1", pb[t][:])

        def put_rb(t):
            put(ub[t], "n2", rb[t][:])

        def make_z(t):
            other = floats("other_%d" % t, S)
            larger = floats("larger_%d" % t, S)
            width = W if t == PACK - 1 else S
            for first in range(0, S, width):
                cols = slice(first, first + width)
                fetch(other[:, cols], ub[t], entries("n3", first, width))
                nc.vector.scalar_tensor_tensor(larger[:, cols], other[:, cols], 0.5, ub[t][:, cols], ALU.mult, ALU.max)
                nc.vector.tensor_scalar_mul(
                    z[:, first * PACK + t : (first + width) * PACK : PACK], larger[:, cols], gain[:, t : t + 1]
                )

        h[0] = leave_bank("h_0", banks1[0], True)
        pair_up(0)
        put_pb(0)
        for t in range(1, PACK):
            h[t] = leave_bank("h_%d" % t, banks1[t], t == 1)
        for t in range(1, PACK):
            pair_up(t)
        second_words((("two", 0), ("hy", 0)), x_table, "picked_words")
        second_bytes("words_offs")
        second_words((("k4", 0), ("k5", 0), ("k3", 0)), d_table, "words_hz")
        put_rb(0)
        put_pb(1)
        make_z(0)
        put_pb(2)
        put_rb(1)
        put_pb(3)
        put_rb(2)
        make_z(1)
        make_z(2)
        put_rb(3)
        make_z(3)
        for half in range(2):
            cols = slice(half * W, (half + 1) * W)
            nc.vector.quantize_mx(
                out=z_words[:, cols].bitcast(FP8X4), scales=z_bytes[:, cols], in_=z[:, half * W * PACK : (half + 1) * W * PACK]
            )
        second_words((("k4", 1), ("k5", 1), ("k3", 1)), d_table, "z")

        h2, ra, rb2, ub2 = {}, {}, {}, {}

        def second_product(u):
            half, cols = u // 2, slice((u % 2) * P, (u % 2 + 1) * P)
            bank = psum.tile([P, S], F32, name="bank2_%d" % u)

            def stationary(name):
                return dict(lhsT=second[name, half][:, cols].bitcast(FP8X4), lhsT_scale=scale_rows[name][:, u * P : (u + 1) * P])

            for coded, moving in (("k4", "two"), ("k5", "hy")):
                nc.tensor.matmul_mx(
                    out=bank[:], rhs=second[moving, 0].bitcast(FP8X4), rhs_scale=scale_rows[moving],
                    start=(coded == "k4"), stop=False, **stationary(coded)
                )
            for part in range(2):
                places = slice(part * W, (part + 1) * W)
                nc.tensor.matmul_mx(
                    out=bank[:, places], rhs=z_words[:, places].bitcast(FP8X4), rhs_scale=z_bytes[:, places],
                    start=False, stop=(part == 1), **stationary("k3")
                )
            h2[u] = leave_bank("h2_%d" % u, bank, u < 2)

        def pair_up2(u):
            pa2 = floats("pa2_%d" % u, W)
            pb2 = floats("pb2_%d" % u, W)
            ra[u] = floats("ra_%d" % u, W)
            rb2[u] = floats("rb2_%d" % u, W)
            ub2[u] = floats("ub2_%d" % u, S)
            fetch(pa2[:], h2[u], lists["n4"][:])
            fetch(pb2[:], h2[u], lists["n5"][:])
            nc.vector.tensor_tensor(ra[u][:], pa2[:], pb2[:], ALU.max)
            nc.vector.tensor_tensor(rb2[u][:], pa2[:], pb2[:], ALU.min)

        def finish(u):
            put(ub2[u], "n7", rb2[u][:])
            result = floats("result_%d" % u, S)
            nc.vector.tensor_sub(result[:], ub2[u][:], h2[u][:])
            nc.sync.dma_start(out[u * P : (u + 1) * P, :], result[:])

        second_product(0)
        second_product(1)
        pair_up2(0)
        pair_up2(1)
        second_product(2)
        second_product(3)
        for first in (0, 2):
            if first:
                pair_up2(first)
                pair_up2(first + 1)
            put(ub2[first], "n6", ra[first][:])
            put(ub2[first + 1], "n6", ra[first + 1][:])
            finish(first)
            finish(first + 1)
